import numpy as np, ml_dtypes
CORES = [3,11,19,27,35,43,51,59]
N = 8
BF = ml_dtypes.bfloat16
def gentries(a):
    return np.ascontiguousarray(a.reshape(8, 16, -1).transpose(0, 2, 1)).reshape(8, -1)
def gtable(e):
    e = np.asarray(e); return np.ascontiguousarray(e.reshape(8, -1, 16).transpose(0, 2, 1)).reshape(128, -1).astype(np.int32)
S, RO, M, KS = 768, 3, 8, 8192
W = N * S
def pair(o):
    p = np.empty(W, np.int64); p[o] = o[np.arange(W) ^ 1]; return p
def match(rng):
    return pair(rng.permutation(W))
def inside(rng):
    return pair(np.concatenate([q * S + rng.permutation(S) for q in range(N)]))
def across(rng):
    return pair(np.stack([np.arange(W // 2), W // 2 + rng.permutation(W // 2)], axis=1).reshape(-1))
def four(o, k):
    p = np.empty(W, np.int64); p[o.reshape(-1)] = o[:, np.arange(4) ^ k].reshape(-1); return p
def eights(rng):
    k = W // 8; i = np.arange(k); z = rng.permutation(np.arange(k, W - 2 * k)).reshape(k, 5)
    o = np.stack([z[:, 0], i, z[:, 1], W - 2 - 2 * i, W - 1 - 2 * i, z[:, 2], z[:, 3], z[:, 4]], axis=1)
    e = np.concatenate([np.full((k, 8), 6), rng.choice(np.array([0, 2, 4]), (k, 7)), np.ones((k, 1), np.int64)], axis=1)
    e = np.take_along_axis(e, np.argsort(rng.random((k, 16)), axis=1), 1)
    lo = rng.integers(0, M - 6, (k, 16)); hi = lo + e; one = lo + (e == 1)
    a = np.empty((16, W), np.int64); a[:, o.reshape(-1)] = np.stack([one, hi, hi, lo, lo, hi, hi, hi], axis=1).reshape(W, 16).T
    return pair(o.reshape(-1)), pair(np.roll(o, -1, axis=1).reshape(-1)), a
def parts(rng):
    share = rng.permutation(np.array([0.1, 0.2, 0.3, 0.5, 0.7, 1.0, 1.0, 1.0])).reshape(8, 1, 1)
    a = rng.integers(0, M, (8, 16, W)); b = np.where(rng.random((8, 16, W)) < share, rng.integers(0, M, (8, 16, W)), 0)
    return a, b, np.stack([match(rng) for g in range(8)]), np.stack([np.stack([match(rng) for t in range(RO)]) for g in range(8)])
def pack(a, b, lk, cd):
    side = lambda v: np.ascontiguousarray(v.reshape(128, N, S).transpose(1, 0, 2)).astype(np.float32).astype(BF)
    return {"x": side(a), "u": side(b), "link": np.stack([gtable(lk[:, q * S:(q + 1) * S]) for q in range(N)]),
            "cand": np.stack([gtable(cd[:, :, q * S:(q + 1) * S].reshape(8, RO * S)) for q in range(N)])}
def setup_inputs(rng):
    return pack(*parts(rng))
def setup_inputs_ties(rng):
    a, b, lk, cd = parts(rng)
    pa = rng.integers(0, M, (8, 16, 4)); pb = rng.integers(0, M, (8, 16, 4))
    pa[2:4] = 0; pa[2:4, 0, 2:] = 1; pb[2:4] = 0
    kind = np.broadcast_to(rng.integers(0, 4, (8, 1, W)), (8, 16, W))
    a[2:] = np.take_along_axis(pa, kind, 2)[2:]; b[2:] = np.take_along_axis(pb, kind, 2)[2:]
    for g in range(2):
        o = rng.permutation(W).reshape(W // 4, 4); lk[g] = four(o, 1)
        for t in range(RO): cd[g, t] = four(o, (2, 3, 1)[t % 3])
    return pack(a, b, lk, cd)
def setup_inputs_again(rng):
    a, b, lk, cd = parts(rng); b = rng.integers(0, 2, b.shape)
    for g in (0, 1): cd[g, 1:] = cd[g, :1]
    for g in (2, 3): cd[g, 0] = lk[g]
    for g in (4, 5): cd[g, 2:] = cd[g, np.arange(2, RO) % 2]
    for g in (6, 7):
        o = rng.permutation(W); lk[g] = pair(o); h = W // 2
        for t in range(RO): cd[g, t] = pair(np.concatenate([o[:h], rng.permutation(o[h:])]))
    return pack(a, b, lk, cd)
def setup_inputs_places(rng):
    a, b, lk, cd = parts(rng); v = np.arange(W)
    lk[0] = v ^ 1; lk[1] = W - 1 - v; lk[2] = (v + W // 2) % W; lk[3] = inside(rng); lk[4] = inside(rng); lk[5] = across(rng)
    for t in range(RO):
        cd[0, t] = W - 1 - v if t % 2 == 0 else v ^ 2
        cd[1, t] = v ^ (1 << (t % 4)); cd[2, t] = inside(rng); cd[3, t] = inside(rng); cd[4, t] = across(rng); cd[5, t] = across(rng)
    o = np.concatenate([np.stack([q * S + rng.permutation(S) for q in four_ranks], axis=1) for four_ranks in rng.permutation(N).reshape(N // 4, 4)])
    lk[7] = four(o, 1); cd[7, 0] = four(o, 2); cd[7, 1] = cd[7, 0]
    p = rng.integers(0, M, (W // 4, 16)); e = (p + rng.integers(M // 4, M - M // 4 + 1, (W // 4, 16))) & (M - 1)
    a[7][:, o.reshape(-1)] = np.stack([p, e, p, e], axis=1).reshape(W, 16).T
    b[6] = rng.integers(0, M, (16, W))
    return pack(a, b, lk, cd)
def setup_inputs_far(rng):
    a, b, lk, cd = parts(rng); v = np.arange(W)
    for g in range(8):
        flip = (rng.random(W) < 0.5)[np.minimum(v, lk[g])]
        s = flip if g % 2 else flip ^ (v < lk[g])
        a[g] = np.where(s, 7, 0)[None, :]
        b[g] = rng.choice(np.array([0, 7]), W)[None, :]
    lk[3], cd[3, 1], a[3] = eights(rng)
    lk[4], last, a[4] = eights(rng); b[4] = 0; cd[4, 1:RO - 1] = lk[4]; cd[4, RO - 1] = last
    o = np.concatenate([np.arange(W // 2).reshape(W // 4, 2), (W // 2 + rng.permutation(W // 2)).reshape(W // 4, 2)], axis=1)
    lk[6] = four(o, 1); cd[6, 1] = four(o, 2); s = np.zeros(W, bool)
    s[o.reshape(-1)] = ((rng.random((W // 4, 1)) < 0.5) ^ (np.arange(4) % 2 == 1)[None, :]).reshape(-1)
    a[6] = np.where(s, 7, 0)[None, :]
    a[7] = rng.integers(0, M, (16, 1)); b[7] = 0
    cd[:, 0] = lk
    return pack(a, b, lk, cd)
def setup_inputs_spread(rng):
    a, b, lk, cd = parts(rng)
    a = np.minimum((np.exp2(3 * rng.random((8, 1, W))) * rng.random(a.shape) * 1.25).astype(np.int64), M - 1)
    b = np.minimum((np.exp2(3 * rng.random((8, 1, W))) * rng.random(b.shape) ** 2).astype(np.int64), M - 1) * (rng.random((8, 1, W)) < 0.75)
    return pack(a, b, lk, cd)
def joined(a, n):
    e = np.stack([gentries(b) for b in a]).astype(np.int64).reshape(N, 8, n, S)
    return np.ascontiguousarray(e.transpose(1, 2, 0, 3)).reshape(8, n, W)
def check_inputs(d):
    bad = []
    for k in ("x", "u"):
        a = np.asarray(d[k]).astype(np.float32)
        if not np.all((a >= 0) & (a <= M - 1) & (a == np.floor(a))): bad.append("range of " + k)
    for k, n in (("link", 1), ("cand", RO)):
        a = np.asarray(d[k])
        if np.min(a) < 0 or np.max(a) > W - 1: bad.append("range of " + k); continue
        e = joined(a, n); v = np.arange(W)
        if np.any(e == v): bad.append("a satellite paired with itself in " + k)
        if np.any(np.take_along_axis(e, e, 2) != v): bad.append("pairs of " + k)
    return bad
def pick(a, i):
    return np.take_along_axis(a, i, 1) if a.ndim == 2 else np.take_along_axis(a, i[:, None, :], 2)
def cost(a, b):
    e = np.abs(a - b)
    return np.add.reduce(e * e, axis=1)
def reference(x, u, link, cand):
    xs, us = [np.ascontiguousarray(a.astype(np.float32).astype(np.int64).transpose(1, 0, 2)).reshape(8, 16, W) for a in (x, u)]
    lk = joined(link, 1)[:, 0]; cd = joined(cand, RO); v = np.arange(W)
    for t in range(RO):
        b = lk; c = cd[:, t]; d = pick(lk, c)
        xb = pick(xs, b); xc = pick(xs, c); xd = pick(xs, d)
        g = cost(xs, xb) + cost(xc, xd) - cost(xs, xc) - cost(xb, xd)
        key = KS * g - np.minimum(v, c)
        go = (g > 0) & (key > pick(key, b)) & (key > pick(key, d))
        new = np.where(go, c, np.where(pick(go, b), pick(d, b), b))
        ch = np.roll(new != lk, -1, axis=0).astype(np.int64)
        xs = (xs + us * ch[:, None, :]) & (M - 1)
        lk = new
    return {"ylink": np.stack([gtable(lk[:, q * S:(q + 1) * S]) for q in range(N)]).astype(np.float32)}

from concourse.bass import DstId, RemoteDMATransfer
from concourse.mybir import AluOpType as A, ActivationFunctionType as F

N, S, W, RO = 8, 768, 6144, 3
f32, bf, i32, u16, f16 = "float32", "bfloat16", "int32", "uint16", "float16"


def _sb(n, d):
    return ("sbuf", [128, n], d)


SCRATCH = {
    "sx": ("dram", [N, 128, 96], bf), "s12": ("dram", [N, 128, 192], bf),
    "sl": ("dram", [N, 128, 24], i32), "rl": ("dram", [N, 128, 24], i32),
    "sf": ("dram", [N, 128, 6], f32), "rf": ("dram", [N, 128, 6], f32),
    "hx": ("dram", [128, 96], bf), "h12": ("dram", [128, 192], bf),
    "hb": _sb(S, bf), "hb12": _sb(2 * S, bf),
    "xtab": _sb(3 * W, bf), "xs": _sb(S, bf), "us": _sb(S, bf), "x12": _sb(2 * S, bf), "m8": _sb(S, bf),
    "xv": _sb(S, bf), "xc": _sb(S, bf), "xd": _sb(S, bf), "t2": _sb(S, bf), "pr": _sb(S, bf),
    "ci": _sb(128, i32), "ci2": _sb(128, i32), "eye": _sb(W, bf),
    "idp": _sb(128, bf), "idn": _sb(128, bf), "gi": _sb(8, i32), "gi2": _sb(8, i32), "gm": _sb(8, f32),
    "bo1": _sb(8, bf), "bo2": _sb(8, bf), "sel": _sb(1024, f32), "selh": _sb(1024, f16), "selb": _sb(1024, bf),
    "pcol": _sb(8, i32), "pf": _sb(16, f32), "c3": _sb(8, f32), "fl": _sb(12, f32), "flu": _sb(12, u16),
    "own0": _sb(48, f32), "own1": _sb(48, i32), "idtab": _sb(384, f32),
    "lk": _sb(48, i32), "cd": _sb(144, i32), "cf": _sb(144, f32),
    "ltab": _sb(384, f32), "ctab": _sb(384, f32), "mtab": _sb(384, f32), "dtab": _sb(384, f32),
    "ktab": _sb(384, f32), "ftab": _sb(384, f32), "ntab": _sb(384, bf),
    "mc": _sb(S, bf), "mb": _sb(S, bf), "md": _sb(S, bf), "mf": _sb(S, bf),
    "ga": _sb(S, f32), "gb": _sb(S, f32), "ge": _sb(S, f32), "gn": _sb(S, bf), "gd": _sb(S, bf),
    "ub": _sb(96, u16), "uc": _sb(96, u16), "ud": _sb(96, u16), "uf": _sb(96, u16),
    "ev": _sb(48, u16), "eb": _sb(48, u16), "ec": _sb(48, u16), "ed": _sb(48, u16),
    "b0": _sb(48, f32), "b1": _sb(48, f32), "d1": _sb(48, f32), "d0": _sb(48, f32), "f0": _sb(48, f32),
    "n1": _sb(48, f32), "a1": _sb(48, f32), "a2": _sb(48, f32),
    "tv": _sb(48, f32), "tc": _sb(48, f32), "tb": _sb(48, f32), "td": _sb(48, f32),
    "g16": _sb(48, f16), "k0": _sb(48, f32), "kb0": _sb(48, f32), "cmb": _sb(48, f32), "fmb": _sb(48, f32),
    "m1": _sb(48, f32), "m2": _sb(48, f32), "go": _sb(48, f32), "gob": _sb(48, f32), "nb1": _sb(48, f32),
    "chs0": _sb(48, bf), "chs1": _sb(48, bf), "chr0": _sb(48, bf), "chr1": _sb(48, bf),
}
BANKS = ("pa", "pb", "pk", "p0", "p1", "p2", "px0", "px1")
for _n in BANKS:
    SCRATCH[_n] = ("psum", [128, 512], f32)

SEMAPHORES = ["pe", "dve", "act", "gp", "stl", "stx", "ldx", "own0", "own12", "st12", "ownl", "ldl", "ldc", "stf", "ownf",
              "out", "sent", "arrl", "arrx", "arr12", "arrf", "arrn0", "arrn1", "harr", "harr12", "hrep", "hrep12"]
CH3 = ((0, 16, "a"), (16, 32, "b"), (32, 48, "c"))
CH2 = ((0, 32, "ab"), (32, 48, "c"))
CH1 = ((0, 48, "abc"),)


def _dst(topo, c):
    rid, pid, _ = topo.addr(c)
    return DstId(rid=rid, pnc=pid)


def _helpers(topo, cores, r):
    free = [c for c in topo.cores_of(cores[r]) if c not in cores]
    return dict(zip([q for q in range(N) if q != r], free))


def _hand_on_engines(topo, src, dst):
    return topo.engines(src, dst)[::2]


def helper_program(g, core, T, topo, r, q):
    sem = T.sem
    rid, pid, _ = topo.addr(T.cores[r])
    eng = _hand_on_engines(topo, core, T.cores[r])
    for land, buf, arr, rep in ((T.hx, T.hb, sem.harr, sem.hrep), (T.h12, T.hb12, sem.harr12, sem.hrep12)):
        for k, qu in enumerate((g.sync, g.scalar)):
            qu.wait_ge(arr, 1)
            for a in range(4 * k, 4 * k + 4):
                qu.dma_start(buf[16 * a:16 * a + 16, :], land[:]).then_inc(rep, 16)
    g.wait_ge(sem.hrep, 128)
    g.remote_dma(T.xtab[:, q * S:(q + 1) * S], T.hb[:], sem.arrx, sem.sent, pid, rid, sum(1 << e for e in eng))
    g.wait_ge(sem.hrep12, 128)
    h = len(eng) // 2
    g.remote_dma_fused([RemoteDMATransfer(
        dst_ids=[_dst(topo, T.cores[r])], dma_engine_mask=sum(1 << e for e in eng[v * h:(v + 1) * h]), remote_sem=sem.arr12,
        src=T.hb12[:, v * S:(v + 1) * S], dst=T.xtab[:, (v + 1) * W + q * S:(v + 1) * W + (q + 1) * S]) for v in range(2)],
        local_sem=sem.sent)
    g.wait_ge(sem.sent, 2 * len(eng))


def rank_program(g, core, T, topo):
    cores = list(T.cores)
    r = T.rank_of(core)
    if r is None:
        for rr in range(N):
            for q, c in _helpers(topo, cores, rr).items():
                if c == core:
                    helper_program(g, core, T, topo, rr, q)
        return
    sem = T.sem
    Q = {"pe": g.tensor, "dve": g.vector, "act": g.scalar, "gp": g, "sp": g.sync}
    cnt, waited, wr, rd = {}, {q: {} for q in Q}, {}, {}

    def wait(q, tok):
        if waited[q].get(tok[0], 0) < tok[1]:
            Q[q].wait_ge(sem[tok[0]], tok[1])
            waited[q][tok[0]] = tok[1]

    def order(q, reads, writes):
        toks = []
        for k in reads:
            toks += wr.get(k, [])
            if k in BANKS:
                toks += [t for t in rd.get(k, []) if t[0] != q]
        for k in writes:
            toks += [t for t in wr.get(k, []) + rd.get(k, []) if not (q == "pe" and t[0] == "pe")]
        best = {}
        for s, v in toks:
            best[s] = max(best.get(s, 0), v)
        for s, v in best.items():
            wait(q, (s, v))

    def note(tok, reads, writes):
        for k in reads:
            rd.setdefault(k, []).append(tok)
        for k in writes:
            wr[k] = [tok]
            rd[k] = []

    def op(q, call, reads, writes):
        order(q, reads, writes)
        cnt[q] = cnt.get(q, 0) + 1
        call().then_inc(sem[q], 1)
        note((q, cnt[q]), reads, writes)

    def dma(q, s, out, in_, reads, writes):
        order(q, reads, writes)
        cnt[s] = cnt.get(s, 0) + 16
        Q[q].dma_start(out, in_).then_inc(sem[s], 16)
        note((s, cnt[s]), reads, writes)

    def arrive(key, s, n):
        cnt[s] = n
        wr.setdefault(key, []).append((s, n))

    V, ACT, PE = g.vector, g.scalar, g.tensor

    def ts(out, in0, s1, s2, o0, o1, reads, writes):
        if o1 is None:
            op("dve", lambda: V.tensor_scalar(out, in0, s1, None, o0), reads, writes)
        else:
            op("dve", lambda: V.tensor_scalar(out, in0, s1, s2, o0, o1), reads, writes)

    def tt(out, a, b, o, reads, writes):
        op("dve", lambda: V.tensor_tensor(out, a, b, o), reads, writes)

    def cp(out, in_, reads, writes):
        op("dve", lambda: V.tensor_copy(out, in_), reads, writes)

    def ac(out, in_, reads, writes, func=F.Copy):
        op("act", lambda: ACT.activation(out, in_, func), reads, writes)

    def mm(out, lhsT, rhs, reads, writes, start=True, stop=True):
        op("pe", lambda: PE.matmul(out, lhsT, rhs, start, stop), reads, writes)

    def fused(srcs, dsts, to, s, reads):
        order("gp", reads, [])
        peers = [q for q in range(N) if q != r]
        g.remote_dma_fused([RemoteDMATransfer(
            dst_ids=[_dst(topo, to(q))], dma_engine_mask=1 << topo.engines(core, to(q))[k], remote_sem=sem[s],
            src=srcs(q), dst=dsts(q)) for k, q in enumerate(peers)], local_sem=sem.sent)
        cnt["sent"] = cnt.get("sent", 0) + len(peers)

    def keys(name, tag):
        return [name + t for t in tag]

    rows = slice(16 * r, 16 * r + 16)
    dma("sp", "stl", T.sl[:, 0:32, :], T.link[:], [], ["sl0"])
    dma("act", "stl", T.sl[:, 32:128, :], T.cand[:], [], ["sl1"])
    wr["sl0"] = wr["sl1"]
    dma("sp", "stx", T.sx[:], T.x[:], [], ["sx"])
    dma("act", "ownl", T.rl[r, 0:32, :], T.link[rows, :], [], ["rl"])
    dma("act", "ownl", T.rl[r, 32:128, :], T.cand[rows, :], [], ["rl2"])
    wr["rl"] = list(wr["rl2"])
    dma("sp", "ldx", T.xs[:], T.x[:], [], ["xs"])
    dma("sp", "ldx", T.us[:], T.u[:], [], ["us"])
    wr["xs"] = wr["us"]
    handed = sum(len(_hand_on_engines(topo, c, core)) for c in _helpers(topo, cores, r).values())
    arrive("rl", "arrl", N - 1)

    def iota(out, pat, base, cm, key, small=False):
        if small:
            op("gp", lambda: g.iota(out, pat, base, cm, allow_small_or_imprecise_dtypes=True), [], [key])
        else:
            op("gp", lambda: g.iota(out, pat, base, cm), [], [key])

    iota(T.ci[:], [[-1, 128]], 128, 1, "ci")
    iota(T.gi[:], [[-16, 8]], 128, 1, "gi")
    iota(T.pcol[:, 0:1], [[0, 1]], 0, 1, "p")
    iota(T.c3[:, 0:3], [[1, 3]], 0, 0, "c3", True)
    iota(T.own0[:], [[16, 48]], 0, 1, "own0i", True)
    iota(T.own1[:], [[128, 6], [768, 8]], 0, 1, "own1")
    fused(lambda q: T.sl[q], lambda q: T.rl[r], lambda q: cores[q], "arrl", ["sl0"])
    fused(lambda q: T.sx[q], lambda q: T.hx[:], lambda q: _helpers(topo, cores, q)[r], "harr", ["sx"])
    iota(T.idtab[:], [[16, 384]], 0, 1, "idtabi", True)

    ts(T.ci2[:], T.ci[:], 15, None, A.bitwise_and, None, ["ci"], ["ci2"])
    ts(T.gi2[:], T.gi[:], 4, None, A.arith_shift_right, None, ["gi"], ["gi2"])
    ts(T.eye[:, 0:128], T.ci2[:], 0.0, None, A.is_equal, None, ["ci2"], ["e128"])
    ts(T.gm[:], T.gi2[:], 8.0, None, A.is_equal, None, ["gi2"], ["gm"])
    for n in (128, 256, 512, 1024, 2048):
        ac(T.eye[:, n:2 * n], T.eye[:, 0:n], ["e%d" % n], ["e%d" % (2 * n)])
    ac(T.eye[:, 4096:W], T.eye[:, 0:2048], ["e2048"], ["e6144"])
    EYE = ["e4096", "e6144"]
    ts(T.pcol[:, 1:2], T.pcol[:, 0:1], 4, None, A.arith_shift_right, None, ["p"], ["p1_"])
    ts(T.pcol[:, 2:3], T.pcol[:, 0:1], 7, None, A.bitwise_and, None, ["p"], ["p2_"])
    ts(T.pcol[:, 3:4], T.pcol[:, 0:1], 3, 1, A.arith_shift_right, A.bitwise_and, ["p"], ["p3_"])
    ts(T.idp[:], T.ci[:], 128.0, None, A.is_equal, None, ["ci"], ["idp"])
    cp(T.pf[:, 0:4], T.pcol[:, 0:4], ["p", "p1_", "p2_", "p3_"], ["pf"])
    ts(T.idn[:], T.ci[:], 128.0, -1.0, A.is_equal, A.mult, ["ci"], ["idn"])
    pf = T.pf
    op("dve", lambda: V.memset(T.fl[:], 0.0), [], ["fl0", "fl1", "fl2"])
    ts(pf[:, 4:5], pf[:, 2:3], 6.0, pf[:, 3:4], A.mult, A.add, ["pf"], ["pf4"])
    ts(pf[:, 6:7], pf[:, 1:2], 32.0, pf[:, 0:1], A.mult, A.add, ["pf"], ["pf6"])
    ts(pf[:, 7:8], pf[:, 1:2], 752.0, None, A.mult, None, ["pf"], ["pf7"])
    ts(pf[:, 8:9], pf[:, 1:2], -16.0, None, A.mult, None, ["pf"], ["pf8"])
    op("act", lambda: ACT.activation(T.idtab[:], T.idtab[:], F.Identity, bias=pf[:, 8:9]), ["idtabi", "pf8"], ["idtab"])
    cp(T.ev[:], T.own1[:], ["own1"], ["ev"])
    ts(pf[:, 5:6], pf[:, 4:5], 8.0, pf[:, 1:2], A.mult, A.add, ["pf", "pf4"], ["pf5"])
    ts(T.fl[:, 0:3], T.c3[:, 0:3], 16.0, pf[:, 6:7], A.mult, A.add, ["c3", "pf6"], ["fl0"])
    ts(T.fl[:, 8:11], T.c3[:, 0:3], 2.0, pf[:, 4:5], A.mult, A.add, ["c3", "pf4"], ["fl2"])
    ts(T.fl[:, 4:7], T.c3[:, 0:3], 16.0, pf[:, 5:6], A.mult, A.add, ["c3", "pf5"], ["fl1"])
    ts(T.own0[:], T.own0[:], pf[:, 7:8], None, A.add, None, ["own0i", "pf7"], ["own0"])
    cp(T.bo1[:], T.gm[:], ["gm"], ["bo1"])
    ts(T.bo2[:], T.gm[:], 2.0, None, A.mult, None, ["gm"], ["bo2"])
    cp(T.flu[:], T.fl[:], ["fl0", "fl1", "fl2"], ["flu"])

    def selector(buf, name, w):
        for s in range(8):
            ts(buf[:, 128 * s:128 * s + 128], T.eye[:, 0:128], T.gm[:, s:s + 1], w, A.mult, A.mult, ["e128", "gm"], [name + str(s)])

    selector(T.sel, "sel", 1.0)
    to0, to1, perm = T.flu[:, 0:3], T.flu[:, 4:7], T.flu[:, 8:11]
    PX = {"a": ("px0", 0, 512), "b": ("px1", 512, 768)}
    PY = {"a": "px0", "b": "px1", "c": "pk"}

    def drift(src, skey, v):
        for t in "ab":
            pk, c0, c1 = PX[t]
            mm(T[pk][:, 0:c1 - c0], T.idp[:], src[:, c0:c1], ["idp"] + skey(t), [pk], True, False)
            mm(T[pk][:, 0:c1 - c0], T.idp[:], T.us[:, c0:c1], ["us"], [pk], False, True)
        for t in "ab":
            pk, c0, c1 = PX[t]
            ts(T.m8[:, c0:c1], T[pk][:, 0:c1 - c0], 8.0, 8.0, A.is_ge, A.mult, [pk], ["m8" + t])
        for t in "ab":
            pk, c0, c1 = PX[t]
            tt(T.x12[:, v * S + c0:v * S + c1], T[pk][:, 0:c1 - c0], T.m8[:, c0:c1], A.subtract, [pk, "m8" + t], ["x12%d%s" % (v, t)])

    drift(T.xs, lambda t: ["xs"], 0)
    drift(T.x12, lambda t: ["x120" + t], 1)
    selector(T.selb, "selb", float(W))
    dma("sp", "ldl", T.lk[:], T.rl[:, 0:32, :], ["rl"], ["lk"])
    dma("sp", "ldc", T.cd[:], T.rl[:, 32:128, :], ["rl"], ["cd"])
    for a in range(8):
        dma("sp", "own0", T.xtab[16 * a:16 * a + 16, r * S:(r + 1) * S], T.x[rows, :], [], ["o0%d" % a])
    wr["x0"] = list(wr["o07"])
    arrive("x0", "arrx", handed)
    X12 = ["x120a", "x120b", "x121a", "x121b"]
    dma("sp", "st12", T.s12[:], T.x12[:], X12, ["s12"])
    fused(lambda q: T.s12[q], lambda q: T.h12[:], lambda q: _helpers(topo, cores, q)[r], "harr12", ["s12"])
    for v in range(2):
        for a in range(8):
            dma("sp", "own12", T.xtab[16 * a:16 * a + 16, (v + 1) * W + r * S:(v + 1) * W + (r + 1) * S],
                T.x12[rows, v * S:(v + 1) * S], X12, ["o12%d%d" % (v, a)])
    wr["xl"] = list(wr["o1217"])
    arrive("xl", "arr12", handed)

    def build(bank, val, vkey, lay, sk="sel"):
        for s in range(8):
            out = T[bank][:, 48 * s:48 * s + 48] if lay == 0 else T[bank][:, s:384:8]
            mm(out, T[sk][:, 128 * s:128 * s + 128], val, [sk + str(s)] + vkey, [bank])

    def whole(u, ukey, src, skeys):
        cp(u[:, 48:96], src, skeys, [ukey + "n"])

    def high(u, ukey, src, skeys):
        ts(u[:, 0:48], src, 1.0 / 16, -15.0 / 32, A.mult, A.add, skeys, [ukey + "h"])

    def split(u, ukey, src, skeys):
        whole(u, ukey, src, skeys)
        high(u, ukey, src, skeys)

    def mask(m, mkey, u, ukey, chunks=CH1):
        for a, b, t in chunks:
            ac(m[:, 16 * a:16 * b], T.eye[:].indirect(u[:, 48 + a:48 + b]), EYE + [ukey + "n"], keys(mkey, t))

    def fold(bank, G, gkey, rkey, lay, a, b, t):
        for blk in range(a // 8, b // 8):
            out = T[bank][:, blk:48:6] if lay == 0 else T[bank][:, 8 * blk:8 * blk + 8]
            mm(out, G[:, 128 * blk:128 * blk + 128], T[rkey][:], keys(gkey, t) + [rkey], [bank])

    def look(bank, tkey, ukey, mkey, gkey, rkey, lay, chunks=CH2):
        for a, b, t in chunks:
            tt(T[gkey][:, 16 * a:16 * b], T[tkey][:].indirect(T[ukey][:, a:b]), T[mkey][:, 16 * a:16 * b], A.mult,
               [tkey, ukey + "h"] + keys(mkey, t), keys(gkey, t))
            fold(bank, T[gkey], gkey, rkey, lay, a, b, t)

    def hold(mkey, banks):
        for (a, b, t), pk in zip(CH2, banks):
            mm(T[pk][:, 0:16 * (b - a)], T.idp[:], T[mkey][:, 16 * a:16 * b], ["idp"] + keys(mkey, t), [pk])

    def fetch(tkey, ukey, gkey, chunks):
        for a, b, t in chunks:
            ac(T[gkey][:, 16 * a:16 * b], T[tkey][:].indirect(T[ukey][:, a:b]), [tkey, ukey + "h"], [gkey + t])

    def keep(bank, gkey, banks, chunks, rkey="gm"):
        for a, b, t in chunks:
            pk, o = (banks[0], 16 * a) if a < 32 else (banks[1], 0)
            tt(T[gkey][:, 16 * a:16 * b], T[pk][:, o:o + 256], T[gkey][:, 16 * a:16 * b], A.mult, [pk, gkey + t], [gkey + t])
            fold(bank, T[gkey], gkey, rkey, 1, a, b, t)

    def xrows(name, lst, lkey, c0, xwin, xk, chunks=CH2):
        for a, e, h in chunks:
            ac(T[name][:, 16 * a:16 * e], xwin.indirect(lst[:, c0 + a:c0 + e]), xk + [lkey], keys(name, h))

    def less_xv(first):
        for a, e, h in CH3:
            mm(T[PY[h]][:, 0:256], T.idn[:], T.xv[:, 16 * a:16 * e], ["idn", "xv" + h], [PY[h]], first, not first)

    B = [(T.b0, "b0"), (T.b1, "b1")]
    cp(T.b0[:], T.lk[:], ["lk"], ["b0"])
    split(T.uc, "uc", T.cd[:, 0:48], ["cd"])
    cp(T.cf[:], T.cd[:], ["cd"], ["cf"])
    for t in range(RO):
        b, bk = B[t % 2]
        nb, nk = B[(t + 1) % 2]
        cft = T.cf[:, 48 * t:48 * t + 48]
        xwin, xk = T.xtab[:, 0:(t + 1) * W], (["x0"] if t == 0 else ["x0", "xl"])
        build("pa", b[:], [bk], 0)
        if t == 0:
            build("pb", cft, ["cf"], 0)
            selector(T.selh, "selh", 8192.0)
        else:
            split(T.uc, "uc", T.ctab[:].indirect(to1), ["ctab", "flu"])
        mask(T.mc, "mc", T.uc, "uc", CH2)
        if t > 0:
            tt(T.mtab[:], T.pb[:, 0:384], T.idtab[:], A.min, ["pb", "idtab"], ["mtab"])
        tt(T.cmb[:], cft, b[:], A.subtract, ["cf", bk], ["cmb"])
        cp(T.ltab[:], T.pa[:, 0:384], ["pa"], ["ltab"])
        if t == 0:
            split(T.ub, "ub", T.ltab[:].indirect(to1), ["ltab", "flu"])
            mask(T.mb, "mb", T.ub, "ub")
            look("p0", "ltab", "uc", "mc", "ga", "gm", 0, CH3)
            ac(T.ctab[:], T.pb[:, 0:384], ["pb"], ["ctab"])
            cp(T.d1[:], T.p0[:, 0:48], ["p0"], ["d1"])
            cp(T.ec[:], T.ctab[:].indirect(to1), ["ctab", "flu"], ["ec"])
            build("pa", T.d1[:], ["d1"], 1)
            split(T.ud, "ud", T.d1[:].indirect(perm), ["d1", "flu"])
            mask(T.md, "md", T.ud, "ud")
            tt(T.mtab[:], T.pb[:, 0:384], T.idtab[:], A.min, ["pb", "idtab"], ["mtab"])
            cp(T.dtab[:], T.pa[:, 0:384], ["pa"], ["dtab"])
            look("p1", "dtab", "ub", "mb", "gb", "gm", 1)
            xrows("xc", T.ec, "ec", 0, xwin, xk)
            cp(T.xv[:, 0:256], xwin.indirect(T.ev[:, 0:16]), xk + ["ev"], ["xva"])
            cp(T.f0[:], T.p1[:, 0:48], ["p1"], ["f0"])
            build("pa", T.f0[:], ["f0"], 0)
            cp(T.xv[:, 256:512], xwin.indirect(T.ev[:, 16:32]), xk + ["ev"], ["xvb"])
            lb, lbk, ld, ldk, c0 = T.ub, "ubn", T.ud, "udn", 48
        else:
            nr, nrk = T["chr%d" % (t - 1)], "chr%d" % (t - 1)
            arrive(nrk, "arrn%d" % (t - 1), len(topo.engines(cores[(r + 1) % N], core)))
            look("p0", "ltab", "uc", "mc", "ga", "gm", 1, CH2[:1])
            split(T.ub, "ub", T.ltab[:].indirect(to1), ["ltab", "flu"])
            mask(T.mb, "mb", T.ub, "ub")
            build("pb", nr[:], [nrk], 0, "selb")
            look("p0", "ltab", "uc", "mc", "ga", "gm", 1, CH2[1:])
            hold("mc", ("px0",))
            cp(T.ntab[:], T.pb[:, 0:384], ["pb"], ["ntab"])
            ac(T.d0[:], T.p0[:, 0:48], ["p0"], ["d0"])
            build("pa", T.d0[:], ["d0"], 0)
            tt(T.tv[:], T.ntab[:].indirect(to0), T.own0[:], A.add, ["ntab", "flu", "own0"], ["tv"])
            fetch("ntab", "uc", "gn", CH3[:1])
            look("p1", "ntab", "uc", "mc", "gn", "bo1", 1, CH3[1:])
            cp(T.ev[:], T.tv[:], ["tv"], ["ev"])
            keep("p1", "gn", ("px0",), CH3[:1], "bo1")
            ac(T.n1[:], T.ntab[:].indirect(to1), ["ntab", "flu"], ["n1"])
            xrows("xv", T.ev, "ev", 0, xwin, xk, CH1)
            tt(T.dtab[:], T.pa[:, 0:384], T.ntab[:], A.add, ["pa", "ntab"], ["dtab"])
            tt(T.tc[:], T.p1[:, 0:48], cft, A.add, ["p1", "cf"], ["tc"])
            tt(T.d1[:], T.dtab[:].indirect(to1), T.n1[:], A.subtract, ["dtab", "flu", "n1"], ["d1"])
            cp(T.ec[:], T.tc[:], ["tc"], ["ec"])
            split(T.ud, "ud", T.d1[:], ["d1"])
            mask(T.md, "md", T.ud, "ud", CH2)
            xrows("xc", T.ec, "ec", 0, xwin, xk)
            look("p0", "dtab", "ub", "mb", "gb", "gm", 1)
            less_xv(True)
            look("p1", "ntab", "ud", "md", "gd", "bo1", 1, CH2[:1])
            ts(T.a1[:], T.p0[:, 0:48], float(W), float(W), A.is_ge, A.mult, ["p0"], ["a1"])
            if t > 1:
                ts(T.a2[:], T.p0[:, 0:48], 2.0 * W, float(W), A.is_ge, A.mult, ["p0"], ["a2"])
            look("p1", "ntab", "ud", "md", "gd", "bo1", 1, CH2[1:])
            if t > 1:
                tt(T.a1[:], T.a1[:], T.a2[:], A.add, ["a1", "a2"], ["a1"])
            tt(T.f0[:], T.p0[:, 0:48], T.a1[:], A.subtract, ["p0", "a1"], ["f0"])
            build("pa", T.f0[:], ["f0"], 0)
            tt(T.td[:], T.p1[:, 0:48], T.d0[:], A.add, ["p1", "d0"], ["td"])
            tt(T.tb[:], T.a1[:], b[:], A.add, ["a1", bk], ["tb"])
            cp(T.ed[:], T.td[:], ["td"], ["ed"])
            cp(T.eb[:], T.tb[:], ["tb"], ["eb"])
            lb, lbk, ld, ldk, c0 = T.eb, "eb", T.ed, "ed", 0
        xrows("xd", ld, ldk, c0, xwin, xk, CH3)
        for a, e, h in CH3:
            mm(T[PY[h]][:, 0:256], T.idp[:], T.xd[:, 16 * a:16 * e], ["idp", "xd" + h], [PY[h]], t == 0, t > 0)
        if t == 0:
            xrows("xv", T.ev, "ev", 0, xwin, xk, CH3[2:])
            less_xv(False)
        for a, e, h in CH2:
            tt(T.t2[:, 16 * a:16 * e], xwin.indirect(lb[:, c0 + a:c0 + e]), T.xc[:, 16 * a:16 * e], A.subtract,
               xk + [lbk] + keys("xc", h), keys("t2", h))
        lay = 1 if t == 0 else 0
        ac(T.ftab[:], T.pa[:, 0:384], ["pa"], ["ftab"])
        for a, e, h in CH3:
            if h == "c":
                whole(T.uf, "uf", T.ftab[:].indirect(to1), ["ftab", "flu"])
                mask(T.mf, "mf", T.uf, "uf", CH2)
            tt(T.pr[:, 16 * a:16 * e], T[PY[h]][:, 0:256], T.t2[:, 16 * a:16 * e], A.mult, [PY[h], "t2" + h], ["pr" + h])
            fold("p2", T.pr, "pr", "bo2", lay, a, e, h)
        cp(T.g16[:], T.p2[:, 0:48], ["p2"], ["g16"])
        build("pk", T.g16[:], ["g16"], 1 - lay, "selh")
        hold("mb", ("px0", "px1"))
        high(T.uf, "uf", T.ftab[:].indirect(to1), ["ftab", "flu"])
        tt(T.fmb[:], T.f0[:], b[:], A.subtract, ["f0", bk], ["fmb"])
        tt(T.ktab[:], T.pk[:, 0:384], T.mtab[:], A.subtract, ["pk", "mtab"], ["ktab"])
        fetch("ktab", "ub", "ga", CH3)
        fetch("ktab", "uf", "ge", CH3)
        hold("mf", ("pa", "pk"))
        if t + 1 < RO:
            build("pb", T.cf[:, 48 * t + 48:48 * t + 96], ["cf"], 0)
        look("p1", "ktab", "ud", "md", "gb", "gm", 1)
        ts(T.k0[:], T.ktab[:].indirect(to0), 0.0, None, A.max, None, ["ktab", "flu"], ["k0"])
        keep("p0", "ga", ("px0", "px1"), CH3)
        ac(T.kb0[:], T.p0[:, 0:48], ["p0"], ["kb0"], F.Relu)
        tt(T.m1[:], T.p1[:, 0:48], T.k0[:], A.is_lt, ["p1", "k0"], ["m1"])
        keep("p2", "ge", ("pa", "pk"), CH3)
        if t + 1 < RO:
            ac(T.ctab[:], T.pb[:, 0:384], ["pb"], ["ctab"])
        tt(T.go[:], T.k0[:], T.kb0[:], A.is_gt, ["k0", "kb0"], ["go"])
        tt(T.go[:], T.go[:], T.m1[:], A.mult, ["go", "m1"], ["go"])
        tt(T.m2[:], T.p2[:, 0:48], T.k0[:], A.max, ["p2", "k0"], ["m2"])
        tt(T.cmb[:], T.cmb[:], T.go[:], A.mult, ["cmb", "go"], ["cmb"])
        if t == 1:
            tt(T.go[:], T.go[:], T.chs0[:], A.add, ["go", "chs0"], ["go"])
        tt(T.gob[:], T.kb0[:], T.m2[:], A.is_gt, ["kb0", "m2"], ["gob"])
        tt(T.nb1[:], T.cmb[:], b[:], A.add, ["cmb", bk], ["nb1"])
        if t + 1 < RO:
            cs = "chs%d" % t
            tt(T[cs][:], T.go[:], T.gob[:], A.add, ["go", "gob"], [cs])
            to = cores[(r - 1) % N]
            rid, pid, _ = topo.addr(to)
            order("gp", [cs], [])
            g.remote_dma(T["chr%d" % t][:], T[cs][:], sem["arrn%d" % t], sem.sent, pid, rid, topo.mask(core, to))
            cnt["sent"] += len(topo.engines(core, to))
        tt(T.fmb[:], T.fmb[:], T.gob[:], A.mult, ["fmb", "gob"], ["fmb"])
        tt(nb[:], T.nb1[:], T.fmb[:], A.add, ["nb1", "fmb"], [nk])

    b, bk = B[RO % 2]
    dma("sp", "stf", T.sf[:], b[:], [bk], ["sf"])
    fused(lambda q: T.sf[q], lambda q: T.rf[r], lambda q: cores[q], "arrf", ["sf"])
    dma("act", "ownf", T.rf[r], b[rows, :], [bk], ["rf"])
    arrive("rf", "arrf", N - 1)
    dma("sp", "out", T.ylink[:], T.rf[:], ["rf"], ["y"])
    for s, v in cnt.items():
        if not any(waited[q].get(s, 0) >= v for q in Q):
            wait("gp", (s, v))
